import numpy as np
import ml_dtypes


def mxq(x, axis, fmt="e4m3"):
    dtype, down = {"e4m3": (ml_dtypes.float8_e4m3fn, 7), "e5m2": (ml_dtypes.float8_e5m2, 14)}[fmt]
    v = np.moveaxis(np.asarray(x, np.float32).astype(ml_dtypes.bfloat16).astype(np.float64), axis, -1)
    blocks = v.reshape(v.shape[:-1] + (-1, 32))
    amax = np.abs(blocks).max(-1, keepdims=True)
    byte = np.maximum(np.where(amax > 0, np.frexp(amax)[1] - 1 + 127, 0) - down, 1)
    scale = np.exp2(byte - 127.0)
    codes = (blocks / scale).astype(np.float32).astype(dtype).astype(np.float64)
    return np.moveaxis((codes * scale).reshape(v.shape), -1, axis)


WIDE = False


def mx_kscale(k):
    if not WIDE:
        return np.ones(k)
    levels = np.array([10, -10, 5, -5, 0])
    if k % 512:
        return np.exp2(np.random.permutation(np.resize(levels, k // 32))).repeat(32)
    a = np.empty((k // 512, 16))
    for p in range(k // 512):
        a[p, :8] = np.random.permutation(np.resize(levels, 8))
        for g in range(8):
            far = levels[np.abs(levels - a[p, g]) >= 10]
            a[p, g + 8] = far[np.random.randint(len(far))]
    return np.exp2(a.ravel()).repeat(32)


def f64(x):
    return np.asarray(x).astype(np.float64)


def striped(idx):
    return np.tile(idx.reshape(-1, 16).T, (8, 1)).astype(np.uint16)


def unstriped(offs):
    return offs[:16].T.reshape(-1).astype(np.int64)


E2M1 = np.array([0.0, 0.5, 1.0, 1.5, 2.0, 3.0, 4.0, 6.0, -0.0, -0.5, -1.0, -1.5, -2.0, -3.0, -4.0, -6.0])


def pack_weight(w, fmt):
    k, n = w.shape
    w = f64(np.asarray(w, np.float32).astype(ml_dtypes.bfloat16)).reshape(k // 32, 32, n)
    amax = np.abs(w).max(1)
    if fmt == "e4m3":
        byte = np.frexp(amax)[1] - 1 + 127 - 7
    else:
        mant, ex = np.frexp(amax / 6.0)
        byte = np.where(mant > 0.5, ex, ex - 1) + 127
    byte = np.clip(np.where(amax > 0, byte, 1), 1, 254)
    scaled = (w * np.exp2(127.0 - byte)[:, None, :]).reshape(k, n).astype(np.float32)
    by_word = np.ascontiguousarray(scaled.reshape(k // 512, 128, 4, n).transpose(0, 1, 3, 2))
    if fmt == "e4m3":
        words = by_word.astype(ml_dtypes.float8_e4m3fn).view(np.uint8)
    else:
        c = by_word.astype(ml_dtypes.float4_e2m1fn).view(np.uint8) & 0xF
        words = (c[..., 0::2] | (c[..., 1::2] << 4)).reshape(k // 512, 128, 2 * n)
    return np.ascontiguousarray(words), np.ascontiguousarray(byte.astype(np.uint8).reshape(k // 512, 16, n))


def unpack_weight(words, scales, fmt):
    g, _, n = scales.shape
    words = np.ascontiguousarray(words).reshape(g, 128, n, -1)
    if fmt == "e4m3":
        vals = words.view(ml_dtypes.float8_e4m3fn).astype(np.float64)
    else:
        nib = np.empty((g, 128, n, 4), np.uint8)
        nib[..., 0::2] = words & 0xF
        nib[..., 1::2] = words >> 4
        vals = E2M1[nib]
    vals = vals * np.repeat(np.exp2(scales.astype(np.float64) - 127.0), 8, axis=1)[..., None]
    return vals.transpose(0, 1, 3, 2).reshape(g * 512, n)


def gelu(v):
    return 0.5 * v * (1.0 + np.tanh(np.sqrt(2.0 / np.pi) * (v + 0.044715 * v**3)))


def twice(P):
    return np.random.permutation(np.repeat(np.arange(P), 2))


K, T, S, P, H, H2 = 1024, 4096, 1024, 512, 1024, 2048


def setup_inputs():
    n = np.random.standard_normal
    s = mx_kscale(K)[:, None]
    u = mx_kscale(H)[:, None]
    d = {}
    d["tab_words"], d["tab_scales"] = pack_weight(n((K, T)) * s, "e4m3")
    d["offs"] = striped(np.random.permutation(T)[:S])
    d["pos1"] = striped(np.random.permutation(S)[:P])
    d["pos2"] = striped(np.random.permutation(S)[:P])
    d["pos3"] = striped(twice(P))
    d["wa"] = (n((K, H)) * 1.5 / K ** 0.5 / s).astype(np.float32)
    d["wb_words"], d["wb_scales"] = pack_weight(n((K, H)) * 1.5 / K ** 0.5 / s, "e4m3")
    d["gain"] = (np.exp(0.3 * n(H)) * u[:, 0]).astype(np.float32)
    d["w4_words"], d["w4_scales"] = pack_weight(n((H, H)) * 1.2 / H ** 0.5 / u ** 2, "e2m1")
    d["cut"] = (np.random.uniform(0.5, 1.2, H) / u[:, 0]).astype(np.float32)
    return d


def reference(tab_words, tab_scales, offs, pos1, pos2, pos3, wa, wb_words, wb_scales, gain, w4_words, w4_scales, cut):
    v = unpack_weight(tab_words, tab_scales, "e4m3")[:, unstriped(offs)]
    both = np.zeros((H2, S))
    both[:H] = mxq(f64(wa), 0, "e4m3").T @ v
    both[H:] = unpack_weight(wb_words, wb_scales, "e4m3").T @ v
    t = np.tanh(both)
    h = f64(gain)[:, None] * (t[:H] + t[H:])
    z = h[:, unstriped(pos1)] * h[:, unstriped(pos2)]
    y = unpack_weight(w4_words, w4_scales, "e2m1").T @ mxq(z, 0, "e4m3")
    up = np.abs(y[:, unstriped(pos3)])
    return up - f64(cut)[:, None] * h

@@ -1,0 +1,283 @@
+from contextlib import ExitStack
+
+import concourse.mybir as mybir
+
+K, T, S, M, H = 1024, 4096, 1024, 512, 1024
+FLOPS = 2 * (2 * K * H * S + H * H * M)
+
+F32 = mybir.dt.float32
+BF16 = mybir.dt.bfloat16
+I32 = mybir.dt.int32
+U32 = mybir.dt.uint32
+U16 = mybir.dt.uint16
+U8 = mybir.dt.uint8
+FP8X4 = mybir.dt.float8_e4m3fn_x4
+FP4X4 = mybir.dt.float4_e2m1fn_x4
+ACT = mybir.ActivationFunctionType
+ALU = mybir.AluOpType
+
+P = 128
+PACK = 4
+PASS = P * PACK
+PASSES = K // PASS
+BLOCKS = H // PASS
+BANK = 512
+HALVES = S // BANK
+QUADS = 4
+Y_COLS = S + 16
+Y_BUFS = 3
+TAB_ROW = 8
+
+
+def tile_list_gait_harmony_scorer_kernel(
+    tc, tab_words, tab_scales, offs, pos1, pos2, pos3, wa, wb_words, wb_scales, gain, w4_words, w4_scales, cut, out
+):
+    nc = tc.nc
+    slices = [(b, t) for b in range(BLOCKS) for t in range(PACK)]
+
+    with ExitStack() as ctx:
+        lists = ctx.enter_context(tc.tile_pool(name="lists", bufs=1))
+        keep = ctx.enter_context(tc.tile_pool(name="keep", bufs=1))
+        ring = ctx.enter_context(tc.tile_pool(name="ring", bufs=2))
+        psum = ctx.enter_context(tc.psum_pool(name="psum", bufs=1))
+
+        def kept(name, shape, dtype):
+            return keep.tile(shape, dtype, name=name, align_bytes=64)
+
+        def load_list(name, src):
+            tile = lists.tile(list(src.shape), U16, name=name)
+            nc.sync.dma_start(tile[:], src)
+            return tile
+
+        tab_sc = keep.tile([P, T], U8, name="tab_sc", tag="tab_sc", align_bytes=64)
+        nc.vector.memset(tab_sc[:].bitcast(I32), 0)
+        w_sc_raw = kept("w_sc_raw", [P, H], U8)
+        nc.vector.memset(w_sc_raw[:].bitcast(I32), 0)
+        warm = kept("warm", [P, 1], F32)
+        nc.vector.memset(warm[:], 0.0)
+        nc.scalar.activation(out=warm[:], in_=warm[:], func=ACT.Tanh)
+
+        offs_t = load_list("offs_t", offs)
+        tab = []
+
+        def load_tab(a):
+            tile = ring.tile([P, T], I32, name="tab%d" % a, tag="big", align_bytes=64)
+            nc.sync.dma_start(tile[:], tab_words[a].rearrange("p t i -> p (t i)").bitcast(I32))
+            tab.append(tile)
+
+        def load_scale_rows(tile, src):
+            for q in range(QUADS):
+                rows = slice(32 * q + TAB_ROW, 32 * q + TAB_ROW + 4 * PASSES)
+                nc.sync.dma_start(tile[rows, :].bitcast(I32), src[:, 4 * q : 4 * q + 4, :].bitcast(I32))
+
+        gain_t = kept("gain_t", [P, BLOCKS, PACK], F32)
+        nc.sync.dma_start(gain_t[:], gain.rearrange("(b p t) -> p b t", b=BLOCKS, t=PACK))
+        load_tab(0)
+        load_scale_rows(tab_sc, tab_scales)
+        load_tab(1)
+        load_scale_rows(w_sc_raw, wb_scales)
+
+        wb_view = wb_words.rearrange("a p c i -> p a (c i)")
+        wb_raw, wa_raw = [], {}
+        for b in range(BLOCKS):
+            tile = kept("wb_raw%d" % b, [P, PASSES, PASS], I32)
+            nc.sync.dma_start(tile[:], wb_view[:, :, 4 * PASS * b : 4 * PASS * (b + 1)].bitcast(I32))
+            wb_raw.append(tile)
+            for a in range(PASSES):
+                tile = ring.tile([P, PACK, PASS], F32, name="wa_raw%d%d" % (b, a), tag="stage", bufs=4, align_bytes=64)
+                src = wa[PASS * a : PASS * (a + 1), PASS * b : PASS * (b + 1)]
+                nc.sync.dma_start(tile[:], src.rearrange("(p i) c -> p i c", i=PACK))
+                wa_raw[b, a] = tile
+            if b == 0:
+                pos1_t = load_list("pos1_t", pos1)
+                pos2_t = load_list("pos2_t", pos2)
+        w4_raw = kept("w4_raw", [P, PASSES, 2 * H], U8)
+        nc.sync.dma_start(w4_raw[:].bitcast(I32), w4_words.rearrange("a p c -> p a c").bitcast(I32))
+        pos3_t = load_list("pos3_t", pos3)
+        w4_sc_raw = kept("w4_sc_raw", [P, PASSES, H], U8)
+        nc.vector.memset(w4_sc_raw[:].bitcast(I32), 0)
+        for q in range(QUADS):
+            src = w4_scales[:, 4 * q : 4 * q + 4, :].rearrange("a r c -> r a c")
+            nc.sync.dma_start(w4_sc_raw[32 * q : 32 * q + 4].bitcast(I32), src.bitcast(I32))
+        cut_t = kept("cut_t", [P, BLOCKS, PACK], F32)
+        nc.sync.dma_start(cut_t[:], cut.rearrange("(b p t) -> p b t", b=BLOCKS, t=PACK))
+        y_win = []
+        for i in range(Y_BUFS):
+            tile = kept("y_win%d" % i, [P, Y_COLS], F32)
+            nc.vector.memset(tile[:, M:], 0.0)
+            y_win.append(tile)
+
+        gain_sq = kept("gain_sq", [P, len(slices), M], F32)
+        for s, (b, t) in enumerate(slices):
+            nc.scalar.activation(
+                out=gain_sq[:, s, :], in_=gain_t[:, b, t : t + 1].to_broadcast([P, M]), func=ACT.Square
+            )
+
+        v_words, v_sc = {}, []
+        per_half = BANK // 16
+
+        def gather_words(a):
+            for jh in range(HALVES):
+                name = "v_words%d%d" % (a, jh)
+                tag = "tab_sc" if (a, jh) == (1, 0) else name
+                tile = keep.tile([P, BANK], U32, name=name, tag=tag, align_bytes=64)
+                picks = offs_t[:, per_half * jh : per_half * (jh + 1)]
+                nc.vector.tensor_copy(tile[:], tab[a][:].bitcast(U32).indirect(picks))
+                v_words[a, jh] = tile
+
+        gather_words(0)
+        for jh in range(HALVES):
+            tile = kept("v_sc%d" % jh, [P, BANK], U8)
+            nc.vector.tensor_copy(tile[:], tab_sc[:].indirect(offs_t[:, per_half * jh : per_half * (jh + 1)]))
+            v_sc.append(tile)
+        w_sc = kept("w_sc", [P, H], U8)
+        nc.vector.tensor_copy(
+            w_sc[:].rearrange("p (b t m) -> p b m t", b=BLOCKS, t=PACK),
+            w_sc_raw[:].rearrange("p (b m t) -> p b m t", b=BLOCKS, t=PACK),
+        )
+        gather_words(1)
+
+        wb_codes, wa_codes, wa_sc = {}, {}, {}
+
+        def deal_wb(b):
+            tile = kept("wb_codes%d" % b, [P, PASSES, PACK, P], I32)
+            nc.vector.tensor_copy(
+                tile[:].rearrange("p a t m -> p a m t"), wb_raw[b][:].rearrange("p a (m t) -> p a m t", t=PACK)
+            )
+            wb_codes[b] = tile
+
+        def quantise_wa(b, a, copy):
+            grouped = ring.tile([P, PACK, P, PACK], BF16, name="wa_grouped", align_bytes=64)
+            copy(grouped[:].rearrange("p t m i -> p m i t"), wa_raw[b, a][:].rearrange("p i (m t) -> p m i t", t=PACK))
+            codes = kept("wa_codes%d%d" % (b, a), [P, PASS], U32)
+            scales = kept("wa_sc%d%d" % (b, a), [P, PASS], U8)
+            nc.vector.quantize_mx(
+                out=codes[:].bitcast(FP8X4), scales=scales[:], in_=grouped[:].rearrange("p t m i -> p (t m i)")
+            )
+            wa_codes[b, a], wa_sc[b, a] = codes, scales
+
+        def tanh_product(dst, weights):
+            for jh in range(HALVES):
+                acc = psum.tile([P, BANK], F32, name="acc1", bufs=5)
+                for a in range(PASSES):
+                    codes, scales = weights(a)
+                    nc.tensor.matmul_mx(
+                        out=acc[:],
+                        lhsT=codes.bitcast(FP8X4),
+                        lhsT_scale=scales,
+                        rhs=v_words[a, jh][:].bitcast(FP8X4),
+                        rhs_scale=v_sc[jh][TAB_ROW + 4 * a :, :],
+                        start=(a == 0),
+                        stop=(a == PASSES - 1),
+                    )
+                nc.scalar.activation(out=dst[:, BANK * jh : BANK * (jh + 1)], in_=acc[:], func=ACT.Tanh)
+
+        u = {}
+
+        def tanh_b(b, t):
+            u[b, t] = kept("u%d%d" % (b, t), [P, S], F32)
+            cols = slice(PASS * b + P * t, PASS * b + P * (t + 1))
+            tanh_product(u[b, t], lambda a: (wb_codes[b][:, a, t, :], w_sc[TAB_ROW + 4 * a :, cols]))
+
+        z = {}
+
+        def tanh_a_and_pairs(b, t, pieces):
+            ta = ring.tile([P, S], F32, name="ta", bufs=3)
+            cols = slice(P * t, P * (t + 1))
+            tanh_product(ta, lambda a: (wa_codes[b, a][:, cols], wa_sc[b, a][:, cols]))
+            nc.vector.tensor_tensor(u[b, t][:], u[b, t][:], ta[:], ALU.add)
+            if t == 0:
+                z[b] = ring.tile([P, PACK, M], F32, name="z%d" % b, tag="big", align_bytes=64)
+            width = M // pieces
+            for i in range(pieces):
+                ms = slice(width * i, width * (i + 1))
+                picks = slice(width * i // 16, width * (i + 1) // 16)
+                left = ring.tile([P, width], F32, name="left", align_bytes=64)
+                nc.vector.tensor_tensor(
+                    left[:], u[b, t][:].indirect(pos1_t[:, picks]), gain_sq[:, PACK * b + t, ms], ALU.mult
+                )
+                nc.vector.tensor_tensor(z[b][:, t, ms], u[b, t][:].indirect(pos2_t[:, picks]), left[:], ALU.mult)
+
+        deal_wb(0)
+        for t in range(PACK):
+            tanh_b(0, t)
+        for a in range(PASSES):
+            quantise_wa(0, a, nc.vector.tensor_copy)
+        deal_wb(1)
+        tanh_a_and_pairs(0, 0, 1)
+        tanh_a_and_pairs(0, 1, 1)
+        quantise_wa(1, 0, nc.scalar.copy)
+        tanh_a_and_pairs(0, 2, 1)
+        quantise_wa(1, 1, nc.scalar.copy)
+        tanh_a_and_pairs(0, 3, 1)
+        for t in range(PACK):
+            tanh_b(1, t)
+            tanh_a_and_pairs(1, t, 2 if t == PACK - 1 else 1)
+
+        w4_codes, w4_sc = {}, {}
+
+        def deal_w4(b, pool, tag):
+            cols = slice(PASS * b, PASS * (b + 1))
+            codes = pool.tile([P, PASSES, 2 * PASS], U8, name="w4_codes%d" % b, tag=tag, align_bytes=64)
+            nc.vector.tensor_copy(
+                codes[:].bitcast(U16).rearrange("p a (t m) -> p a m t", t=PACK),
+                w4_raw[:].bitcast(U16)[:, :, cols].rearrange("p a (m t) -> p a m t", t=PACK),
+            )
+            scales = pool.tile([P, PASSES, PASS], U8, name="w4_sc%d" % b, tag=tag, align_bytes=64)
+            nc.vector.tensor_copy(
+                scales[:].rearrange("p a (t m) -> p a m t", t=PACK),
+                w4_sc_raw[:, :, cols].rearrange("p a (m t) -> p a m t", t=PACK),
+            )
+            w4_codes[b], w4_sc[b] = codes, scales
+
+        deal_w4(0, ring, "w4_first")
+        neg_cg = kept("neg_cg", [P, BLOCKS, PACK], F32)
+        nc.vector.scalar_tensor_tensor(
+            out=neg_cg[:], in0=cut_t[:], scalar=-1.0, in1=gain_t[:], op0=ALU.mult, op1=ALU.mult
+        )
+
+        z_codes, z_sc = [], []
+        half = M // 2
+        for b in range(BLOCKS):
+            codes = kept("z_codes%d" % b, [P, M], U32)
+            scales = kept("z_sc%d" % b, [P, M], U8)
+            for i in range(2):
+                ms = slice(half * i, half * (i + 1))
+                grouped = ring.tile([P, half, PACK], BF16, name="z_grouped", bufs=4, align_bytes=64)
+                copy = nc.vector.tensor_copy if (b, i) == (BLOCKS - 1, 1) else nc.scalar.copy
+                copy(
+                    grouped[:].rearrange("p (c i) t -> p c t i", i=4),
+                    z[b][:, :, ms].rearrange("p t (c i) -> p c t i", i=4),
+                )
+                nc.vector.quantize_mx(
+                    out=codes[:, ms].bitcast(FP8X4), scales=scales[:, ms], in_=grouped[:].rearrange("p m t -> p (m t)")
+                )
+            z_codes.append(codes)
+            z_sc.append(scales)
+
+        deal_w4(1, ring, "left")
+
+        out_rows = out.rearrange("(b p t) j -> b t p j", b=BLOCKS, t=PACK)
+        for s, (b, t) in enumerate(slices):
+            nc.scalar.activation(out=u[b, t][:], in_=u[b, t][:], func=ACT.Copy, scale=neg_cg[:, b, t : t + 1])
+            acc = psum.tile([P, M], F32, name="acc2", bufs=3)
+            for a in range(BLOCKS):
+                nc.tensor.matmul_mx(
+                    out=acc[:],
+                    lhsT=w4_codes[b][:, a, 2 * P * t : 2 * P * (t + 1)].bitcast(FP4X4),
+                    lhsT_scale=w4_sc[b][:, a, P * t : P * (t + 1)],
+                    rhs=z_codes[a][:].bitcast(FP8X4),
+                    rhs_scale=z_sc[a][:],
+                    start=(a == 0),
+                    stop=(a == BLOCKS - 1),
+                )
+            window = y_win[s % Y_BUFS]
+            nc.scalar.activation(out=window[:, :M], in_=acc[:], func=ACT.Abs)
+            result = ring.tile([P, S], F32, name="result", tag="stage", bufs=4, align_bytes=64)
+            pieces = 2 if s == len(slices) - 1 else 1
+            width = S // pieces
+            for i in range(pieces):
+                js = slice(width * i, width * (i + 1))
+                picks = pos3_t[:, width * i // 16 : width * (i + 1) // 16]
+                nc.vector.tensor_tensor(result[:, js], window[:].indirect(picks), u[b, t][:, js], ALU.add)
+                nc.sync.dma_start(out_rows[b, t][:, js], result[:, js])

@@ -24,9 +24,14 @@ BLOCKS = H // PASS
 BANK = 512
 HALVES = S // BANK
 QUADS = 4
-Y_COLS = S + 16
+SCALE_ROWS = 4
+PER_COLUMN = 16
+FIRST_ROW = 8
+Y_COLS = S + PER_COLUMN
 Y_BUFS = 3
-TAB_ROW = 8
+TA_BUFS = 3
+STAGE_BUFS = 4
+BANKS_1, BANKS_2 = 5, 3
 
 
 def tile_list_gait_harmony_scorer_kernel(
@@ -44,100 +49,107 @@ def tile_list_gait_harmony_scorer_kernel(
         def kept(name, shape, dtype):
             return keep.tile(shape, dtype, name=name, align_bytes=64)
 
+        def zeroed_plane(name, columns):
+            tile = kept(name, [P, columns], U8)
+            nc.vector.memset(tile[:].bitcast(I32), 0)
+            return tile
+
         def load_list(name, src):
             tile = lists.tile(list(src.shape), U16, name=name)
             nc.sync.dma_start(tile[:], src)
             return tile
 
-        tab_sc = keep.tile([P, T], U8, name="tab_sc", tag="tab_sc", align_bytes=64)
-        nc.vector.memset(tab_sc[:].bitcast(I32), 0)
-        w_sc_raw = kept("w_sc_raw", [P, H], U8)
-        nc.vector.memset(w_sc_raw[:].bitcast(I32), 0)
+        def entries(list_tile, span):
+            return list_tile[:, span.start // PER_COLUMN : span.stop // PER_COLUMN]
+
+        def pieces(total, count):
+            return [slice(total // count * i, total // count * (i + 1)) for i in range(count)]
+
+        def load_scale_rows(queue, tile, src, row):
+            for q in range(QUADS):
+                rows = slice(32 * q + row, 32 * q + row + SCALE_ROWS * PASSES)
+                queue.dma_start(tile[rows, :].bitcast(I32), src[:, SCALE_ROWS * q : SCALE_ROWS * (q + 1), :].bitcast(I32))
+
+        def load_per_channel(name, src):
+            tile = kept(name, [P, BLOCKS, PACK], F32)
+            nc.sync.dma_start(tile[:], src.rearrange("(b p t) -> p b t", b=BLOCKS, t=PACK))
+            return tile
+
+        def deal_scales(dst, src):
+            nc.vector.tensor_copy(
+                dst[:].rearrange("p (b t m) -> p b m t", b=BLOCKS, t=PACK),
+                src[:].rearrange("p (b m t) -> p b m t", b=BLOCKS, t=PACK),
+            )
+
+        wb_sc_raw = zeroed_plane("wb_sc_raw", H)
+        tab_sc = zeroed_plane("tab_sc", T)
         warm = kept("warm", [P, 1], F32)
         nc.vector.memset(warm[:], 0.0)
         nc.scalar.activation(out=warm[:], in_=warm[:], func=ACT.Tanh)
 
         offs_t = load_list("offs_t", offs)
+        gain_t = load_per_channel("gain_t", gain)
         tab = []
-
-        def load_tab(a):
-            tile = ring.tile([P, T], I32, name="tab%d" % a, tag="big", align_bytes=64)
+        for a in range(PASSES):
+            tile = ring.tile([P, T], I32, name="tab", tag="table", align_bytes=64)
             nc.sync.dma_start(tile[:], tab_words[a].rearrange("p t i -> p (t i)").bitcast(I32))
             tab.append(tile)
+            if a == 0:
+                load_scale_rows(nc.gpsimd, tab_sc, tab_scales, FIRST_ROW)
+        load_scale_rows(nc.sync, wb_sc_raw, wb_scales, FIRST_ROW)
 
-        def load_scale_rows(tile, src):
-            for q in range(QUADS):
-                rows = slice(32 * q + TAB_ROW, 32 * q + TAB_ROW + 4 * PASSES)
-                nc.sync.dma_start(tile[rows, :].bitcast(I32), src[:, 4 * q : 4 * q + 4, :].bitcast(I32))
-
-        gain_t = kept("gain_t", [P, BLOCKS, PACK], F32)
-        nc.sync.dma_start(gain_t[:], gain.rearrange("(b p t) -> p b t", b=BLOCKS, t=PACK))
-        load_tab(0)
-        load_scale_rows(tab_sc, tab_scales)
-        load_tab(1)
-        load_scale_rows(w_sc_raw, wb_scales)
-
-        wb_view = wb_words.rearrange("a p c i -> p a (c i)")
+        wb_bytes = wb_words.rearrange("a p c i -> p a (c i)")
         wb_raw, wa_raw = [], {}
         for b in range(BLOCKS):
             tile = kept("wb_raw%d" % b, [P, PASSES, PASS], I32)
-            nc.sync.dma_start(tile[:], wb_view[:, :, 4 * PASS * b : 4 * PASS * (b + 1)].bitcast(I32))
+            nc.sync.dma_start(tile[:], wb_bytes[:, :, PACK * PASS * b : PACK * PASS * (b + 1)].bitcast(I32))
             wb_raw.append(tile)
             for a in range(PASSES):
-                tile = ring.tile([P, PACK, PASS], F32, name="wa_raw%d%d" % (b, a), tag="stage", bufs=4, align_bytes=64)
+                tile = ring.tile([P, PACK, PASS], F32, name="wa_raw", tag="stage", bufs=STAGE_BUFS, align_bytes=64)
                 src = wa[PASS * a : PASS * (a + 1), PASS * b : PASS * (b + 1)]
                 nc.sync.dma_start(tile[:], src.rearrange("(p i) c -> p i c", i=PACK))
                 wa_raw[b, a] = tile
             if b == 0:
                 pos1_t = load_list("pos1_t", pos1)
                 pos2_t = load_list("pos2_t", pos2)
-        w4_raw = kept("w4_raw", [P, PASSES, 2 * H], U8)
+        w4_raw = kept("w4_raw", [P, BLOCKS, 2 * H], U8)
         nc.sync.dma_start(w4_raw[:].bitcast(I32), w4_words.rearrange("a p c -> p a c").bitcast(I32))
         pos3_t = load_list("pos3_t", pos3)
-        w4_sc_raw = kept("w4_sc_raw", [P, PASSES, H], U8)
-        nc.vector.memset(w4_sc_raw[:].bitcast(I32), 0)
-        for q in range(QUADS):
-            src = w4_scales[:, 4 * q : 4 * q + 4, :].rearrange("a r c -> r a c")
-            nc.sync.dma_start(w4_sc_raw[32 * q : 32 * q + 4].bitcast(I32), src.bitcast(I32))
-        cut_t = kept("cut_t", [P, BLOCKS, PACK], F32)
-        nc.sync.dma_start(cut_t[:], cut.rearrange("(b p t) -> p b t", b=BLOCKS, t=PACK))
-        y_win = []
+        w4_sc_raw = zeroed_plane("w4_sc_raw", H)
+        load_scale_rows(nc.sync, w4_sc_raw, w4_scales, 0)
+        w4_sc_second = zeroed_plane("w4_sc_second", H)
+        cut_t = load_per_channel("cut_t", cut)
+
+        y_windows = []
         for i in range(Y_BUFS):
-            tile = kept("y_win%d" % i, [P, Y_COLS], F32)
+            tile = kept("y_window%d" % i, [P, Y_COLS], F32)
             nc.vector.memset(tile[:, M:], 0.0)
-            y_win.append(tile)
+            y_windows.append(tile)
 
         gain_sq = kept("gain_sq", [P, len(slices), M], F32)
         for s, (b, t) in enumerate(slices):
-            nc.scalar.activation(
-                out=gain_sq[:, s, :], in_=gain_t[:, b, t : t + 1].to_broadcast([P, M]), func=ACT.Square
-            )
+            column = gain_t[:, b, t : t + 1]
+            nc.scalar.activation(out=gain_sq[:, s, :], in_=column.to_broadcast([P, M]), func=ACT.Square)
 
         v_words, v_sc = {}, []
-        per_half = BANK // 16
 
         def gather_words(a):
-            for jh in range(HALVES):
-                name = "v_words%d%d" % (a, jh)
-                tag = "tab_sc" if (a, jh) == (1, 0) else name
-                tile = keep.tile([P, BANK], U32, name=name, tag=tag, align_bytes=64)
-                picks = offs_t[:, per_half * jh : per_half * (jh + 1)]
-                nc.vector.tensor_copy(tile[:], tab[a][:].bitcast(U32).indirect(picks))
+            for jh, js in enumerate(pieces(S, HALVES)):
+                tag = "tab_sc" if (a, jh) == (1, 0) else "v_words%d%d" % (a, jh)
+                tile = keep.tile([P, BANK], U32, name="v_words", tag=tag, align_bytes=64)
+                nc.vector.tensor_copy(tile[:], tab[a][:].bitcast(U32).indirect(entries(offs_t, js)))
                 v_words[a, jh] = tile
 
         gather_words(0)
-        for jh in range(HALVES):
+        for jh, js in enumerate(pieces(S, HALVES)):
             tile = kept("v_sc%d" % jh, [P, BANK], U8)
-            nc.vector.tensor_copy(tile[:], tab_sc[:].indirect(offs_t[:, per_half * jh : per_half * (jh + 1)]))
+            nc.vector.tensor_copy(tile[:], tab_sc[:].indirect(entries(offs_t, js)))
             v_sc.append(tile)
-        w_sc = kept("w_sc", [P, H], U8)
-        nc.vector.tensor_copy(
-            w_sc[:].rearrange("p (b t m) -> p b m t", b=BLOCKS, t=PACK),
-            w_sc_raw[:].rearrange("p (b m t) -> p b m t", b=BLOCKS, t=PACK),
-        )
         gather_words(1)
+        wb_sc = kept("wb_sc", [P, H], U8)
+        deal_scales(wb_sc, wb_sc_raw)
 
-        wb_codes, wa_codes, wa_sc = {}, {}, {}
+        wb_codes, wa_codes, wa_sc, u, z = {}, {}, {}, {}, {}
 
         def deal_wb(b):
             tile = kept("wb_codes%d" % b, [P, PASSES, PACK, P], I32)
@@ -146,108 +158,97 @@ def tile_list_gait_harmony_scorer_kernel(
             )
             wb_codes[b] = tile
 
-        def quantise_wa(b, a, copy):
-            grouped = ring.tile([P, PACK, P, PACK], BF16, name="wa_grouped", align_bytes=64)
-            copy(grouped[:].rearrange("p t m i -> p m i t"), wa_raw[b, a][:].rearrange("p i (m t) -> p m i t", t=PACK))
-            codes = kept("wa_codes%d%d" % (b, a), [P, PASS], U32)
-            scales = kept("wa_sc%d%d" % (b, a), [P, PASS], U8)
+        def quantise_wa(b, a, ts, copy):
+            grouped = ring.tile([P, len(ts), P, PACK], BF16, name="wa_grouped", align_bytes=64)
+            src = wa_raw[b, a][:].rearrange("p i (m t) -> p m i t", t=PACK)[:, :, :, ts.start : ts.stop]
+            copy(grouped[:].rearrange("p t m i -> p m i t"), src)
+            codes = kept("wa_codes%d%d%d" % (b, a, ts.start), [P, len(ts) * P], U32)
+            scales = kept("wa_sc%d%d%d" % (b, a, ts.start), [P, len(ts) * P], U8)
             nc.vector.quantize_mx(
                 out=codes[:].bitcast(FP8X4), scales=scales[:], in_=grouped[:].rearrange("p t m i -> p (t m i)")
             )
-            wa_codes[b, a], wa_sc[b, a] = codes, scales
+            for t, cols in zip(ts, pieces(len(ts) * P, len(ts))):
+                wa_codes[b, a, t], wa_sc[b, a, t] = codes[:, cols], scales[:, cols]
 
         def tanh_product(dst, weights):
-            for jh in range(HALVES):
-                acc = psum.tile([P, BANK], F32, name="acc1", bufs=5)
-                for a in range(PASSES):
-                    codes, scales = weights(a)
+            for jh, js in enumerate(pieces(S, HALVES)):
+                acc = psum.tile([P, BANK], F32, name="acc1", bufs=BANKS_1)
+                for a, (codes, scales) in enumerate(weights):
                     nc.tensor.matmul_mx(
                         out=acc[:],
                         lhsT=codes.bitcast(FP8X4),
                         lhsT_scale=scales,
                         rhs=v_words[a, jh][:].bitcast(FP8X4),
-                        rhs_scale=v_sc[jh][TAB_ROW + 4 * a :, :],
+                        rhs_scale=v_sc[jh][FIRST_ROW + SCALE_ROWS * a :, :],
                         start=(a == 0),
                         stop=(a == PASSES - 1),
                     )
-                nc.scalar.activation(out=dst[:, BANK * jh : BANK * (jh + 1)], in_=acc[:], func=ACT.Tanh)
+                nc.scalar.activation(out=dst[:, js], in_=acc[:], func=ACT.Tanh)
 
-        u = {}
+        def first_stage(s, b, t):
+            u[b, t] = kept("u%d" % s, [P, S], F32)
+            cols = slice(P * s, P * (s + 1))
+            tanh_product(
+                u[b, t], [(wb_codes[b][:, a, t, :], wb_sc[FIRST_ROW + SCALE_ROWS * a :, cols]) for a in range(PASSES)]
+            )
+            ta = ring.tile([P, S], F32, name="ta", bufs=TA_BUFS, align_bytes=64)
+            tanh_product(ta, [(wa_codes[b, a, t], wa_sc[b, a, t]) for a in range(PASSES)])
+            for js in pieces(S, HALVES if s == 0 else 1):
+                nc.vector.tensor_tensor(u[b, t][:, js], u[b, t][:, js], ta[:, js], ALU.add)
 
-        def tanh_b(b, t):
-            u[b, t] = kept("u%d%d" % (b, t), [P, S], F32)
-            cols = slice(PASS * b + P * t, PASS * b + P * (t + 1))
-            tanh_product(u[b, t], lambda a: (wb_codes[b][:, a, t, :], w_sc[TAB_ROW + 4 * a :, cols]))
-
-        z = {}
-
-        def tanh_a_and_pairs(b, t, pieces):
-            ta = ring.tile([P, S], F32, name="ta", bufs=3)
-            cols = slice(P * t, P * (t + 1))
-            tanh_product(ta, lambda a: (wa_codes[b, a][:, cols], wa_sc[b, a][:, cols]))
-            nc.vector.tensor_tensor(u[b, t][:], u[b, t][:], ta[:], ALU.add)
+        def pair_products(s, b, t):
             if t == 0:
-                z[b] = ring.tile([P, PACK, M], F32, name="z%d" % b, tag="big", align_bytes=64)
-            width = M // pieces
-            for i in range(pieces):
-                ms = slice(width * i, width * (i + 1))
-                picks = slice(width * i // 16, width * (i + 1) // 16)
-                left = ring.tile([P, width], F32, name="left", align_bytes=64)
-                nc.vector.tensor_tensor(
-                    left[:], u[b, t][:].indirect(pos1_t[:, picks]), gain_sq[:, PACK * b + t, ms], ALU.mult
-                )
-                nc.vector.tensor_tensor(z[b][:, t, ms], u[b, t][:].indirect(pos2_t[:, picks]), left[:], ALU.mult)
+                z[b] = ring.tile([P, PACK, M], F32, name="z", tag="table", align_bytes=64)
+            for ms in pieces(M, 2 if s == len(slices) - 1 else 1):
+                left = ring.tile([P, ms.stop - ms.start], F32, name="left", align_bytes=64)
+                nc.vector.tensor_tensor(left[:], u[b, t][:].indirect(entries(pos1_t, ms)), gain_sq[:, s, ms], ALU.mult)
+                nc.vector.tensor_tensor(z[b][:, t, ms], u[b, t][:].indirect(entries(pos2_t, ms)), left[:], ALU.mult)
 
         deal_wb(0)
-        for t in range(PACK):
-            tanh_b(0, t)
-        for a in range(PASSES):
-            quantise_wa(0, a, nc.vector.tensor_copy)
-        deal_wb(1)
-        tanh_a_and_pairs(0, 0, 1)
-        tanh_a_and_pairs(0, 1, 1)
-        quantise_wa(1, 0, nc.scalar.copy)
-        tanh_a_and_pairs(0, 2, 1)
-        quantise_wa(1, 1, nc.scalar.copy)
-        tanh_a_and_pairs(0, 3, 1)
-        for t in range(PACK):
-            tanh_b(1, t)
-            tanh_a_and_pairs(1, t, 2 if t == PACK - 1 else 1)
+        quantise_wa(0, 0, range(0, PACK), nc.vector.tensor_copy)
+        quantise_wa(0, 1, range(0, PACK // 2), nc.vector.tensor_copy)
+        quantise_wa(0, 1, range(PACK // 2, PACK), nc.vector.tensor_copy)
+        for s, (b, t) in enumerate(slices):
+            first_stage(s, b, t)
+            pair_products(s, b, t)
+            if s == 0:
+                deal_wb(1)
+            if 1 <= s <= PASSES:
+                quantise_wa(1, s - 1, range(0, PACK), nc.scalar.copy)
 
-        w4_codes, w4_sc = {}, {}
+        w4_codes = {}
 
-        def deal_w4(b, pool, tag):
-            cols = slice(PASS * b, PASS * (b + 1))
-            codes = pool.tile([P, PASSES, 2 * PASS], U8, name="w4_codes%d" % b, tag=tag, align_bytes=64)
+        def deal_w4(b, tag, bufs):
+            codes = ring.tile([P, BLOCKS, 2 * PASS], U8, name="w4_codes", tag=tag, bufs=bufs, align_bytes=64)
             nc.vector.tensor_copy(
                 codes[:].bitcast(U16).rearrange("p a (t m) -> p a m t", t=PACK),
-                w4_raw[:].bitcast(U16)[:, :, cols].rearrange("p a (m t) -> p a m t", t=PACK),
+                w4_raw[:].bitcast(U16)[:, :, PASS * b : PASS * (b + 1)].rearrange("p a (m t) -> p a m t", t=PACK),
             )
-            scales = pool.tile([P, PASSES, PASS], U8, name="w4_sc%d" % b, tag=tag, align_bytes=64)
-            nc.vector.tensor_copy(
-                scales[:].rearrange("p a (t m) -> p a m t", t=PACK),
-                w4_sc_raw[:, :, cols].rearrange("p a (m t) -> p a m t", t=PACK),
-            )
-            w4_codes[b], w4_sc[b] = codes, scales
+            w4_codes[b] = codes
 
-        deal_w4(0, ring, "w4_first")
-        neg_cg = kept("neg_cg", [P, BLOCKS, PACK], F32)
+        w4_sc_first = kept("w4_sc_first", [P, H], U8)
+        deal_scales(w4_sc_first, w4_sc_raw)
+        for q in range(QUADS):
+            rows = slice(32 * q, 32 * q + SCALE_ROWS)
+            below = slice(rows.start + SCALE_ROWS, rows.stop + SCALE_ROWS)
+            nc.sync.dma_start(w4_sc_second[rows, :].bitcast(I32), w4_sc_first[below, :].bitcast(I32))
+        w4_sc = [w4_sc_first, w4_sc_second]
+        deal_w4(0, "w4_first", 1)
+        neg_cut_gain = kept("neg_cut_gain", [P, BLOCKS, PACK], F32)
         nc.vector.scalar_tensor_tensor(
-            out=neg_cg[:], in0=cut_t[:], scalar=-1.0, in1=gain_t[:], op0=ALU.mult, op1=ALU.mult
+            out=neg_cut_gain[:], in0=cut_t[:], scalar=-1.0, in1=gain_t[:], op0=ALU.mult, op1=ALU.mult
         )
 
         z_codes, z_sc = [], []
-        half = M // 2
         for b in range(BLOCKS):
             codes = kept("z_codes%d" % b, [P, M], U32)
             scales = kept("z_sc%d" % b, [P, M], U8)
-            for i in range(2):
-                ms = slice(half * i, half * (i + 1))
-                grouped = ring.tile([P, half, PACK], BF16, name="z_grouped", bufs=4, align_bytes=64)
+            for i, ms in enumerate(pieces(M, 2)):
+                grouped = kept("z_grouped%d%d" % (b, i), [P, M // 2, PACK], BF16)
                 copy = nc.vector.tensor_copy if (b, i) == (BLOCKS - 1, 1) else nc.scalar.copy
                 copy(
-                    grouped[:].rearrange("p (c i) t -> p c t i", i=4),
-                    z[b][:, :, ms].rearrange("p t (c i) -> p c t i", i=4),
+                    grouped[:].rearrange("p (c n) t -> p c t n", n=4),
+                    z[b][:, :, ms].rearrange("p t (c n) -> p c t n", n=4),
                 )
                 nc.vector.quantize_mx(
                     out=codes[:, ms].bitcast(FP8X4), scales=scales[:, ms], in_=grouped[:].rearrange("p m t -> p (m t)")
@@ -255,29 +256,26 @@ def tile_list_gait_harmony_scorer_kernel(
             z_codes.append(codes)
             z_sc.append(scales)
 
-        deal_w4(1, ring, "left")
+        deal_w4(1, "left", 2)
 
         out_rows = out.rearrange("(b p t) j -> b t p j", b=BLOCKS, t=PACK)
         for s, (b, t) in enumerate(slices):
-            nc.scalar.activation(out=u[b, t][:], in_=u[b, t][:], func=ACT.Copy, scale=neg_cg[:, b, t : t + 1])
-            acc = psum.tile([P, M], F32, name="acc2", bufs=3)
+            own = u[b, t]
+            nc.scalar.activation(out=own[:], in_=own[:], func=ACT.Copy, scale=neg_cut_gain[:, b, t : t + 1])
+            acc = psum.tile([P, M], F32, name="acc2", bufs=BANKS_2)
             for a in range(BLOCKS):
                 nc.tensor.matmul_mx(
                     out=acc[:],
                     lhsT=w4_codes[b][:, a, 2 * P * t : 2 * P * (t + 1)].bitcast(FP4X4),
-                    lhsT_scale=w4_sc[b][:, a, P * t : P * (t + 1)],
+                    lhsT_scale=w4_sc[a][:, P * s : P * (s + 1)],
                     rhs=z_codes[a][:].bitcast(FP8X4),
                     rhs_scale=z_sc[a][:],
                     start=(a == 0),
                     stop=(a == BLOCKS - 1),
                 )
-            window = y_win[s % Y_BUFS]
+            window = y_windows[s % Y_BUFS]
             nc.scalar.activation(out=window[:, :M], in_=acc[:], func=ACT.Abs)
-            result = ring.tile([P, S], F32, name="result", tag="stage", bufs=4, align_bytes=64)
-            pieces = 2 if s == len(slices) - 1 else 1
-            width = S // pieces
-            for i in range(pieces):
-                js = slice(width * i, width * (i + 1))
-                picks = pos3_t[:, width * i // 16 : width * (i + 1) // 16]
-                nc.vector.tensor_tensor(result[:, js], window[:].indirect(picks), u[b, t][:, js], ALU.add)
+            result = ring.tile([P, S], F32, name="result", tag="stage", bufs=STAGE_BUFS, align_bytes=64)
+            for js in pieces(S, 2 if s == len(slices) - 1 else 1):
+                nc.vector.tensor_tensor(result[:, js], window[:].indirect(entries(pos3_t, js)), own[:, js], ALU.add)
                 nc.sync.dma_start(out_rows[b, t][:, js], result[:, js])

@@ -65,10 +65,11 @@ def tile_list_gait_harmony_scorer_kernel(
         def pieces(total, count):
             return [slice(total // count * i, total // count * (i + 1)) for i in range(count)]
 
-        def load_scale_rows(queue, tile, src, row):
+        def load_scale_rows(tile, src, row):
             for q in range(QUADS):
                 rows = slice(32 * q + row, 32 * q + row + SCALE_ROWS * PASSES)
-                queue.dma_start(tile[rows, :].bitcast(I32), src[:, SCALE_ROWS * q : SCALE_ROWS * (q + 1), :].bitcast(I32))
+                src_rows = src[:, SCALE_ROWS * q : SCALE_ROWS * (q + 1), :]
+                nc.sync.dma_start(tile[rows, :].bitcast(I32), src_rows.bitcast(I32))
 
         def load_per_channel(name, src):
             tile = kept(name, [P, BLOCKS, PACK], F32)
@@ -81,8 +82,8 @@ def tile_list_gait_harmony_scorer_kernel(
                 src[:].rearrange("p (b m t) -> p b m t", b=BLOCKS, t=PACK),
             )
 
-        wb_sc_raw = zeroed_plane("wb_sc_raw", H)
         tab_sc = zeroed_plane("tab_sc", T)
+        wb_sc_raw = zeroed_plane("wb_sc_raw", H)
         warm = kept("warm", [P, 1], F32)
         nc.vector.memset(warm[:], 0.0)
         nc.scalar.activation(out=warm[:], in_=warm[:], func=ACT.Tanh)
@@ -95,8 +96,8 @@ def tile_list_gait_harmony_scorer_kernel(
             nc.sync.dma_start(tile[:], tab_words[a].rearrange("p t i -> p (t i)").bitcast(I32))
             tab.append(tile)
             if a == 0:
-                load_scale_rows(nc.gpsimd, tab_sc, tab_scales, FIRST_ROW)
-        load_scale_rows(nc.sync, wb_sc_raw, wb_scales, FIRST_ROW)
+                load_scale_rows(tab_sc, tab_scales, FIRST_ROW)
+        load_scale_rows(wb_sc_raw, wb_scales, FIRST_ROW)
 
         wb_bytes = wb_words.rearrange("a p c i -> p a (c i)")
         wb_raw, wa_raw = [], {}
@@ -116,7 +117,7 @@ def tile_list_gait_harmony_scorer_kernel(
         nc.sync.dma_start(w4_raw[:].bitcast(I32), w4_words.rearrange("a p c -> p a c").bitcast(I32))
         pos3_t = load_list("pos3_t", pos3)
         w4_sc_raw = zeroed_plane("w4_sc_raw", H)
-        load_scale_rows(nc.sync, w4_sc_raw, w4_scales, 0)
+        load_scale_rows(w4_sc_raw, w4_scales, 0)
         w4_sc_second = zeroed_plane("w4_sc_second", H)
         cut_t = load_per_channel("cut_t", cut)
 

from contextlib import ExitStack

import concourse.mybir as mybir

K, T, S, M, H = 1024, 4096, 1024, 512, 1024
FLOPS = 2 * (2 * K * H * S + H * H * M)

F32 = mybir.dt.float32
BF16 = mybir.dt.bfloat16
I32 = mybir.dt.int32
U32 = mybir.dt.uint32
U16 = mybir.dt.uint16
U8 = mybir.dt.uint8
FP8X4 = mybir.dt.float8_e4m3fn_x4
FP4X4 = mybir.dt.float4_e2m1fn_x4
ACT = mybir.ActivationFunctionType
ALU = mybir.AluOpType

P = 128
PACK = 4
PASS = P * PACK
PASSES = K // PASS
BLOCKS = H // PASS
BANK = 512
HALVES = S // BANK
QUADS = 4
SCALE_ROWS = 4
PER_COLUMN = 16
FIRST_ROW = 8
Y_COLS = S + PER_COLUMN
Y_BUFS = 3
TA_BUFS = 3
STAGE_BUFS = 4
BANKS_1, BANKS_2 = 5, 3


def tile_list_gait_harmony_scorer_kernel(
    tc, tab_words, tab_scales, offs, pos1, pos2, pos3, wa, wb_words, wb_scales, gain, w4_words, w4_scales, cut, out
):
    nc = tc.nc
    slices = [(b, t) for b in range(BLOCKS) for t in range(PACK)]

    with ExitStack() as ctx:
        lists = ctx.enter_context(tc.tile_pool(name="lists", bufs=1))
        keep = ctx.enter_context(tc.tile_pool(name="keep", bufs=1))
        ring = ctx.enter_context(tc.tile_pool(name="ring", bufs=2))
        psum = ctx.enter_context(tc.psum_pool(name="psum", bufs=1))

        def kept(name, shape, dtype):
            return keep.tile(shape, dtype, name=name, align_bytes=64)

        def zeroed_plane(name, columns):
            tile = kept(name, [P, columns], U8)
            nc.vector.memset(tile[:].bitcast(I32), 0)
            return tile

        def load_list(name, src):
            tile = lists.tile(list(src.shape), U16, name=name)
            nc.sync.dma_start(tile[:], src)
            return tile

        def entries(list_tile, span):
            return list_tile[:, span.start // PER_COLUMN : span.stop // PER_COLUMN]

        def pieces(total, count):
            return [slice(total // count * i, total // count * (i + 1)) for i in range(count)]

        def load_scale_rows(tile, src, row):
            for q in range(QUADS):
                rows = slice(32 * q + row, 32 * q + row + SCALE_ROWS * PASSES)
                src_rows = src[:, SCALE_ROWS * q : SCALE_ROWS * (q + 1), :]
                nc.sync.dma_start(tile[rows, :].bitcast(I32), src_rows.bitcast(I32))

        def load_per_channel(name, src):
            tile = kept(name, [P, BLOCKS, PACK], F32)
            nc.sync.dma_start(tile[:], src.rearrange("(b p t) -> p b t", b=BLOCKS, t=PACK))
            return tile

        def deal_scales(dst, src):
            nc.vector.tensor_copy(
                dst[:].rearrange("p (b t m) -> p b m t", b=BLOCKS, t=PACK),
                src[:].rearrange("p (b m t) -> p b m t", b=BLOCKS, t=PACK),
            )

        tab_sc = zeroed_plane("tab_sc", T)
        wb_sc_raw = zeroed_plane("wb_sc_raw", H)
        warm = kept("warm", [P, 1], F32)
        nc.vector.memset(warm[:], 0.0)
        nc.scalar.activation(out=warm[:], in_=warm[:], func=ACT.Tanh)

        offs_t = load_list("offs_t", offs)
        gain_t = load_per_channel("gain_t", gain)
        tab = []
        for a in range(PASSES):
            tile = ring.tile([P, T], I32, name="tab", tag="table", align_bytes=64)
            nc.sync.dma_start(tile[:], tab_words[a].rearrange("p t i -> p (t i)").bitcast(I32))
            tab.append(tile)
            if a == 0:
                load_scale_rows(tab_sc, tab_scales, FIRST_ROW)
        load_scale_rows(wb_sc_raw, wb_scales, FIRST_ROW)

        wb_bytes = wb_words.rearrange("a p c i -> p a (c i)")
        wb_raw, wa_raw = [], {}
        for b in range(BLOCKS):
            tile = kept("wb_raw%d" % b, [P, PASSES, PASS], I32)
            nc.sync.dma_start(tile[:], wb_bytes[:, :, PACK * PASS * b : PACK * PASS * (b + 1)].bitcast(I32))
            wb_raw.append(tile)
            for a in range(PASSES):
                tile = ring.tile([P, PACK, PASS], F32, name="wa_raw", tag="stage", bufs=STAGE_BUFS, align_bytes=64)
                src = wa[PASS * a : PASS * (a + 1), PASS * b : PASS * (b + 1)]
                nc.sync.dma_start(tile[:], src.rearrange("(p i) c -> p i c", i=PACK))
                wa_raw[b, a] = tile
            if b == 0:
                pos1_t = load_list("pos1_t", pos1)
                pos2_t = load_list("pos2_t", pos2)
        w4_raw = kept("w4_raw", [P, BLOCKS, 2 * H], U8)
        nc.sync.dma_start(w4_raw[:].bitcast(I32), w4_words.rearrange("a p c -> p a c").bitcast(I32))
        pos3_t = load_list("pos3_t", pos3)
        w4_sc_raw = zeroed_plane("w4_sc_raw", H)
        load_scale_rows(w4_sc_raw, w4_scales, 0)
        w4_sc_second = zeroed_plane("w4_sc_second", H)
        cut_t = load_per_channel("cut_t", cut)

        y_windows = []
        for i in range(Y_BUFS):
            tile = kept("y_window%d" % i, [P, Y_COLS], F32)
            nc.vector.memset(tile[:, M:], 0.0)
            y_windows.append(tile)

        gain_sq = kept("gain_sq", [P, len(slices), M], F32)
        for s, (b, t) in enumerate(slices):
            column = gain_t[:, b, t : t + 1]
            nc.scalar.activation(out=gain_sq[:, s, :], in_=column.to_broadcast([P, M]), func=ACT.Square)

        v_words, v_sc = {}, []

        def gather_words(a):
            for jh, js in enumerate(pieces(S, HALVES)):
                tag = "tab_sc" if (a, jh) == (1, 0) else "v_words%d%d" % (a, jh)
                tile = keep.tile([P, BANK], U32, name="v_words", tag=tag, align_bytes=64)
                nc.vector.tensor_copy(tile[:], tab[a][:].bitcast(U32).indirect(entries(offs_t, js)))
                v_words[a, jh] = tile

        gather_words(0)
        for jh, js in enumerate(pieces(S, HALVES)):
            tile = kept("v_sc%d" % jh, [P, BANK], U8)
            nc.vector.tensor_copy(tile[:], tab_sc[:].indirect(entries(offs_t, js)))
            v_sc.append(tile)
        gather_words(1)
        wb_sc = kept("wb_sc", [P, H], U8)
        deal_scales(wb_sc, wb_sc_raw)

        wb_codes, wa_codes, wa_sc, u, z = {}, {}, {}, {}, {}

        def deal_wb(b):
            tile = kept("wb_codes%d" % b, [P, PASSES, PACK, P], I32)
            nc.vector.tensor_copy(
                tile[:].rearrange("p a t m -> p a m t"), wb_raw[b][:].rearrange("p a (m t) -> p a m t", t=PACK)
            )
            wb_codes[b] = tile

        def quantise_wa(b, a, ts, copy):
            grouped = ring.tile([P, len(ts), P, PACK], BF16, name="wa_grouped", align_bytes=64)
            src = wa_raw[b, a][:].rearrange("p i (m t) -> p m i t", t=PACK)[:, :, :, ts.start : ts.stop]
            copy(grouped[:].rearrange("p t m i -> p m i t"), src)
            codes = kept("wa_codes%d%d%d" % (b, a, ts.start), [P, len(ts) * P], U32)
            scales = kept("wa_sc%d%d%d" % (b, a, ts.start), [P, len(ts) * P], U8)
            nc.vector.quantize_mx(
                out=codes[:].bitcast(FP8X4), scales=scales[:], in_=grouped[:].rearrange("p t m i -> p (t m i)")
            )
            for t, cols in zip(ts, pieces(len(ts) * P, len(ts))):
                wa_codes[b, a, t], wa_sc[b, a, t] = codes[:, cols], scales[:, cols]

        def tanh_product(dst, weights):
            for jh, js in enumerate(pieces(S, HALVES)):
                acc = psum.tile([P, BANK], F32, name="acc1", bufs=BANKS_1)
                for a, (codes, scales) in enumerate(weights):
                    nc.tensor.matmul_mx(
                        out=acc[:],
                        lhsT=codes.bitcast(FP8X4),
                        lhsT_scale=scales,
                        rhs=v_words[a, jh][:].bitcast(FP8X4),
                        rhs_scale=v_sc[jh][FIRST_ROW + SCALE_ROWS * a :, :],
                        start=(a == 0),
                        stop=(a == PASSES - 1),
                    )
                nc.scalar.activation(out=dst[:, js], in_=acc[:], func=ACT.Tanh)

        def first_stage(s, b, t):
            u[b, t] = kept("u%d" % s, [P, S], F32)
            cols = slice(P * s, P * (s + 1))
            tanh_product(
                u[b, t], [(wb_codes[b][:, a, t, :], wb_sc[FIRST_ROW + SCALE_ROWS * a :, cols]) for a in range(PASSES)]
            )
            ta = ring.tile([P, S], F32, name="ta", bufs=TA_BUFS, align_bytes=64)
            tanh_product(ta, [(wa_codes[b, a, t], wa_sc[b, a, t]) for a in range(PASSES)])
            for js in pieces(S, HALVES if s == 0 else 1):
                nc.vector.tensor_tensor(u[b, t][:, js], u[b, t][:, js], ta[:, js], ALU.add)

        def pair_products(s, b, t):
            if t == 0:
                z[b] = ring.tile([P, PACK, M], F32, name="z", tag="table", align_bytes=64)
            for ms in pieces(M, 2 if s == len(slices) - 1 else 1):
                left = ring.tile([P, ms.stop - ms.start], F32, name="left", align_bytes=64)
                nc.vector.tensor_tensor(left[:], u[b, t][:].indirect(entries(pos1_t, ms)), gain_sq[:, s, ms], ALU.mult)
                nc.vector.tensor_tensor(z[b][:, t, ms], u[b, t][:].indirect(entries(pos2_t, ms)), left[:], ALU.mult)

        deal_wb(0)
        quantise_wa(0, 0, range(0, PACK), nc.vector.tensor_copy)
        quantise_wa(0, 1, range(0, PACK // 2), nc.vector.tensor_copy)
        quantise_wa(0, 1, range(PACK // 2, PACK), nc.vector.tensor_copy)
        for s, (b, t) in enumerate(slices):
            first_stage(s, b, t)
            pair_products(s, b, t)
            if s == 0:
                deal_wb(1)
            if 1 <= s <= PASSES:
                quantise_wa(1, s - 1, range(0, PACK), nc.scalar.copy)

        w4_codes = {}

        def deal_w4(b, tag, bufs):
            codes = ring.tile([P, BLOCKS, 2 * PASS], U8, name="w4_codes", tag=tag, bufs=bufs, align_bytes=64)
            nc.vector.tensor_copy(
                codes[:].bitcast(U16).rearrange("p a (t m) -> p a m t", t=PACK),
                w4_raw[:].bitcast(U16)[:, :, PASS * b : PASS * (b + 1)].rearrange("p a (m t) -> p a m t", t=PACK),
            )
            w4_codes[b] = codes

        w4_sc_first = kept("w4_sc_first", [P, H], U8)
        deal_scales(w4_sc_first, w4_sc_raw)
        for q in range(QUADS):
            rows = slice(32 * q, 32 * q + SCALE_ROWS)
            below = slice(rows.start + SCALE_ROWS, rows.stop + SCALE_ROWS)
            nc.sync.dma_start(w4_sc_second[rows, :].bitcast(I32), w4_sc_first[below, :].bitcast(I32))
        w4_sc = [w4_sc_first, w4_sc_second]
        deal_w4(0, "w4_first", 1)
        neg_cut_gain = kept("neg_cut_gain", [P, BLOCKS, PACK], F32)
        nc.vector.scalar_tensor_tensor(
            out=neg_cut_gain[:], in0=cut_t[:], scalar=-1.0, in1=gain_t[:], op0=ALU.mult, op1=ALU.mult
        )

        z_codes, z_sc = [], []
        for b in range(BLOCKS):
            codes = kept("z_codes%d" % b, [P, M], U32)
            scales = kept("z_sc%d" % b, [P, M], U8)
            for i, ms in enumerate(pieces(M, 2)):
                grouped = kept("z_grouped%d%d" % (b, i), [P, M // 2, PACK], BF16)
                copy = nc.vector.tensor_copy if (b, i) == (BLOCKS - 1, 1) else nc.scalar.copy
                copy(
                    grouped[:].rearrange("p (c n) t -> p c t n", n=4),
                    z[b][:, :, ms].rearrange("p t (c n) -> p c t n", n=4),
                )
                nc.vector.quantize_mx(
                    out=codes[:, ms].bitcast(FP8X4), scales=scales[:, ms], in_=grouped[:].rearrange("p m t -> p (m t)")
                )
            z_codes.append(codes)
            z_sc.append(scales)

        deal_w4(1, "left", 2)

        out_rows = out.rearrange("(b p t) j -> b t p j", b=BLOCKS, t=PACK)
        for s, (b, t) in enumerate(slices):
            own = u[b, t]
            nc.scalar.activation(out=own[:], in_=own[:], func=ACT.Copy, scale=neg_cut_gain[:, b, t : t + 1])
            acc = psum.tile([P, M], F32, name="acc2", bufs=BANKS_2)
            for a in range(BLOCKS):
                nc.tensor.matmul_mx(
                    out=acc[:],
                    lhsT=w4_codes[b][:, a, 2 * P * t : 2 * P * (t + 1)].bitcast(FP4X4),
                    lhsT_scale=w4_sc[a][:, P * s : P * (s + 1)],
                    rhs=z_codes[a][:].bitcast(FP8X4),
                    rhs_scale=z_sc[a][:],
                    start=(a == 0),
                    stop=(a == BLOCKS - 1),
                )
            window = y_windows[s % Y_BUFS]
            nc.scalar.activation(out=window[:, :M], in_=acc[:], func=ACT.Abs)
            result = ring.tile([P, S], F32, name="result", tag="stage", bufs=STAGE_BUFS, align_bytes=64)
            for js in pieces(S, 2 if s == len(slices) - 1 else 1):
                nc.vector.tensor_tensor(result[:, js], window[:].indirect(entries(pos3_t, js)), own[:, js], ALU.add)
                nc.sync.dma_start(out_rows[b, t][:, js], result[:, js])
